import numpy as np, ml_dtypes
CORES = [56,61,80,85]
N = 4
import mx_ref
NC, G = 384, 4
C, C2 = np.float32(0.019), np.float32(0.029)
CNT = [[96,96,96,96],[96,96,96,96],[96,96,96,96],[96,96,96,96]]
OFF = [[sum(c[:e]) for e in range(N + 1)] for c in CNT]
BF = ml_dtypes.bfloat16
def cut(t, i, w=512):
    return t[:, w * i:w * i + w]
def tile(rs):
    return np.stack(rs, axis=2).reshape(128, -1).astype(BF)
def layer(w, X):
    out = []
    for i in range(G):
        for t in range(len(X)):
            p = mx_ref.matmul(mx_ref.quantize(cut(w, len(X) * i + t)), X[t])
            z = p if t == 0 else z + p
        out.append(z)
    return out
def act(Z):
    return [np.maximum(z, 0) * C for z in Z]
def setup_inputs(rng):
    def f(*shape):
        return mx_ref.flush((rng.standard_normal(shape, dtype=np.float32) * np.exp2(rng.integers(-2, 3, shape[:-1] + (1,)))).astype(BF))
    return {"x": f(N, 128, 4 * NC), "w1": f(N, 128, G * 512), "w2": f(N, 128, G * 512), "w3": f(N, 128, 512)}
def setup_inputs_blocks(rng):
    d = setup_inputs(rng)
    for k in ("x", "w3"): d[k] = mx_ref.spread(d[k], rng, 4)
    for k in ("w1", "w2"): d[k] = mx_ref.spread(d[k], rng, 2)
    return d
def setup_inputs_wide(rng):
    d = setup_inputs(rng)
    for k in ("x", "w1", "w2", "w3"): d[k] = mx_ref.flush((d[k].astype(np.float32) * np.exp2(rng.integers(-4, 5, (N, 1, 1))).astype(np.float32)).astype(BF))
    return d
def setup_inputs_zeros(rng):
    d = setup_inputs(rng); v = d["x"].reshape(N, 128, -1, 4).copy()
    v[np.broadcast_to((rng.random((N, 1, v.shape[2], 1)) < 0.33), v.shape)] = 0
    d["x"] = v.reshape(d["x"].shape)
    return d
def act2(Z):
    return [np.maximum(z, 0) * C2 for z in Z]
def reference(x, w1, w2, w3):
    h = [tile(act(layer(w1[j], [mx_ref.quantize(x[j])]))) for j in range(N)]
    g = []
    for e in range(N):
        t = np.concatenate([h[j][:, 4 * OFF[j][e]:4 * OFF[j][e + 1]] for j in range(N)], axis=1)
        g.append(tile(act2(layer(w2[e], [mx_ref.quantize(t)]))))
    y = np.zeros((N, 128, NC), np.float32)
    for j in range(N):
        back = []
        for e in range(N):
            a = sum(CNT[i][e] for i in range(j))
            back.append(g[e][:, 4 * a:4 * a + 4 * CNT[j][e]])
        y[j] = mx_ref.matmul(mx_ref.quantize(w3[j]), mx_ref.quantize(np.concatenate(back, axis=1)))
    return {"y": y}

@@ -1,0 +1,249 @@
+import numpy as np
+from concourse.bass import DstId, RemoteDMATransfer
+from concourse.mybir import dt, AluOpType, ActivationFunctionType
+
+SIM = 96
+RUN = 96
+HALF = 2 * RUN
+C1 = float(np.float32(0.019))
+C2 = float(np.float32(0.029))
+F8, U8, BF, F32 = "float8_e4m3fn_x4", "uint8", "bfloat16", "float32"
+
+SCRATCH = {
+    "xb": ("sbuf", [128, 1536], BF), "w1b": ("sbuf", [128, 2048], BF),
+    "w2b": ("sbuf", [128, 2048], BF), "w3b": ("sbuf", [128, 512], BF),
+    "xq": ("sbuf", [128, 384], F8), "xs": ("sbuf", [128, 384], U8),
+    "w1q": ("sbuf", [128, 512], F8), "w1s": ("sbuf", [128, 512], U8),
+    "w2q": ("sbuf", [128, 512], F8), "w2s": ("sbuf", [128, 512], U8),
+    "w3q": ("sbuf", [128, 128], F8), "w3s": ("sbuf", [128, 128], U8),
+    "hf": ("sbuf", [128, 4 * HALF], BF), "hn": ("sbuf", [128, 4 * HALF], BF),
+    "gf": ("sbuf", [128, 4 * HALF], BF), "gn": ("sbuf", [128, 4 * HALF], BF),
+    "hfq": ("sbuf", [128, HALF], F8), "hfs": ("sbuf", [128, HALF], U8),
+    "gfq": ("sbuf", [128, HALF], F8), "gfs": ("sbuf", [128, HALF], U8),
+    "bfq": ("sbuf", [128, HALF], F8), "bfs": ("sbuf", [128, HALF], U8),
+    "afq": ("sbuf", [128, HALF], F8), "afs": ("sbuf", [128, HALF], U8),
+    "bnq": ("sbuf", [128, 3 * RUN], F8), "bns": ("sbuf", [128, 3 * RUN], U8),
+    "anq": ("sbuf", [128, 3 * RUN], F8), "ans": ("sbuf", [128, 3 * RUN], U8),
+    "rhq": ("sbuf", [128, RUN], F8), "rhs": ("sbuf", [128, RUN], U8),
+    "rgq": ("sbuf", [128, RUN], F8), "rgs": ("sbuf", [128, RUN], U8),
+    "yn": ("sbuf", [128, HALF], F32), "yf": ("sbuf", [128, HALF], F32),
+}
+for _k in range(8):
+    SCRATCH["ps%d" % _k] = ("psum", [128, 512], F32)
+
+SEMAPHORES = (
+    ["l_xf", "l_xn", "l_w1a", "l_w1b", "l_w2", "l_w3"]
+    + ["q_xf", "q_xn", "q_w3", "q_hf", "q_hn", "q_gf", "q_gn"]
+    + ["q_w1_%d" % i for i in range(4)] + ["q_w2_%d" % i for i in range(4)]
+    + ["m_%s%d" % (t, i) for t in ("hf", "hn", "gf", "gn") for i in range(4)] + ["m_yn", "m_yf"]
+    + ["t_hf", "t_hn", "t_gf", "t_gn"]
+    + ["rhq", "rhs", "rgq", "rgs"]
+    + ["a_bf", "a_bn", "a_af", "a_an"]
+    + ["c_yn", "c_yf", "sent", "st_n", "st_f"])
+
+
+def _bits(mask):
+    return [1 << k for k in range(mask.bit_length()) if mask >> k & 1]
+
+
+def _plan(T, topo):
+    cores = list(T.cores)
+    far, relay = [], {}
+    for s, cs in enumerate(cores):
+        f = [d for d, cd in enumerate(cores) if d != s and not topo.may_write(cs, cd)]
+        cand = [c for c in range(SIM) if T.rank_of(c) is None and topo.chip(c) == topo.chip(cs)
+                and topo.die(c) == topo.die(cs) and all(topo.may_write(c, cores[d]) for d in f)]
+        far.append(f)
+        for i, d in enumerate(f):
+            relay[s, d] = cand[i]
+    return cores, far, relay
+
+
+def _send(g, topo, core, dst, mask, out, in_, rsem, lsem):
+    rid, pid, _ = topo.addr(dst)
+    g.remote_dma(out, in_, rsem, lsem, pid, rid, mask)
+    return len(_bits(mask))
+
+
+def _relay_program(g, core, T, topo, cores, far, s, d):
+    S = T.sem
+    i = far[d].index(s)
+    a, b = RUN * i, RUN * i + RUN
+    dst = cores[d]
+    n_in = _hop1(topo, cores[s], core, far[s].index(d), len(far[s]))
+    n_in = len(_bits(n_in))
+    out_mask = topo.mask(core, dst)
+    sent = 0
+    for q, p, dq, dp, sem in (("rhq", "rhs", "bfq", "bfs", S.a_bf), ("rgq", "rgs", "afq", "afs", S.a_af)):
+        g.wait_ge(S[q], n_in)
+        sent += _send(g, topo, core, dst, out_mask, T[dq][:, a:b].bitcast(dt.uint8), T[q][:].bitcast(dt.uint8), sem, S.sent)
+        g.wait_ge(S[p], n_in)
+        sent += _send(g, topo, core, dst, out_mask, T[dp][:, a:b], T[p][:], sem, S.sent)
+    g.wait_ge(S.sent, sent)
+
+
+def _hop1(topo, src, relay, i, parts):
+    b = _bits(topo.mask(src, relay))
+    n = len(b) // parts
+    return sum(b[i * n:i * n + n])
+
+
+def rank_program(g, core, T, topo):
+    cores, far, relay = _plan(T, topo)
+    rank = T.rank_of(core)
+    S = T.sem
+    if rank is None:
+        for (s, d), c in relay.items():
+            if c == core:
+                _relay_program(g, core, T, topo, cores, far, s, d)
+        return
+
+    me_far = far[rank]
+    group = [r for r in range(len(cores)) if r not in me_far]
+    pos = group.index(rank)
+    peer = group[1 - pos]
+    fo, no = RUN * me_far[0], RUN * group[0]
+    V, SC, TE, SY = g.vector, g.scalar, g.tensor, g.sync
+    relu = ActivationFunctionType.Relu
+    ps = [T["ps%d" % k] for k in range(8)]
+
+    SY.dma_start(T.xb[:, 4 * fo:4 * fo + 4 * HALF], T.x[:, 4 * fo:4 * fo + 4 * HALF]).then_inc(S.l_xf, 16)
+    SC.dma_start(T.w1b[:, 0:1536], T.w1[:, 0:1536]).then_inc(S.l_w1a, 16)
+    SY.dma_start(T.w1b[:, 1536:2048], T.w1[:, 1536:2048]).then_inc(S.l_w1b, 16)
+    SY.dma_start(T.xb[:, 4 * no:4 * no + 4 * HALF], T.x[:, 4 * no:4 * no + 4 * HALF]).then_inc(S.l_xn, 16)
+    SY.dma_start(T.w2b[:], T.w2[:]).then_inc(S.l_w2, 16)
+    SY.dma_start(T.w3b[:], T.w3[:]).then_inc(S.l_w3, 16)
+
+    def quant(q, p, src, c0, c1, e0, sem):
+        V.quantize_mx(T[q][:, c0:c1], T[p][:, c0:c1], T[src][:, e0:e0 + 4 * (c1 - c0)]).then_inc(sem, 1)
+
+    def act(eng, tile, i, bank, c):
+        out, src = T[tile][:, i:4 * HALF:4], ps[bank][:, 0:HALF]
+        eng.wait_ge(S["m_%s%d" % (tile, i)], 1)
+        if eng is SC:
+            SC.activation(out, src, relu, scale=c).then_inc(S["t_" + tile], 1)
+        else:
+            V.tensor_scalar(out, src, 0.0, c, AluOpType.max, AluOpType.mult).then_inc(S["t_" + tile], 1)
+
+    def product(tile, i, bank, w, q, p, c0):
+        TE.matmul_mx(ps[bank][:, 0:HALF], T[w + "q"][:, 128 * i:128 * i + 128], T[w + "s"][:, 128 * i:128 * i + 128],
+                     T[q][:, c0:c0 + HALF], T[p][:, c0:c0 + HALF], True, True).then_inc(S["m_%s%d" % (tile, i)], 1)
+
+    b_q = RUN if pos == 0 else 0
+    b_m = 0 if pos == 0 else RUN
+    a_q, a_m = b_m, b_q
+    b_out = 2 * RUN if pos == 0 else 0
+    a_out = 0 if pos == 0 else 2 * RUN
+    b_land = 2 * RUN if pos == 0 else 0
+    a_land = 0 if pos == 0 else 2 * RUN
+
+    TE.wait_ge(S.q_xf, 1)
+    for i in range(4):
+        TE.wait_ge(S["q_w1_%d" % i], 1)
+        product("hf", i, i, "w1", "xq", "xs", fo)
+    TE.wait_ge(S.q_xn, 1)
+    for i in range(4):
+        product("hn", i, 4 + i, "w1", "xq", "xs", no)
+
+    near_mask = topo.mask(core, cores[peer])
+    near_in = len(_bits(topo.mask(cores[peer], core)))
+    far_in = sum(len(_bits(topo.mask(relay[s, rank], core))) for s in me_far)
+
+    TE.wait_ge(S.t_hf, 4)
+    TE.wait_ge(S.q_hn, 1)
+    TE.wait_ge(S.a_bn, 2 * near_in)
+    for i in range(4):
+        TE.wait_ge(S["q_w2_%d" % i], 1)
+        product("gn", i, i, "w2", "bnq", "bns", b_m)
+    TE.wait_ge(S.t_hn, 4)
+    TE.wait_ge(S.a_bf, 2 * far_in)
+    for i in range(4):
+        product("gf", i, 4 + i, "w2", "bfq", "bfs", 0)
+    TE.wait_ge(S.q_w3, 1)
+    TE.wait_ge(S.t_gn, 4)
+    TE.wait_ge(S.q_gn, 1)
+    TE.wait_ge(S.a_an, 2 * near_in)
+    TE.matmul_mx(ps[0][:, 0:HALF], T.w3q[:], T.w3s[:], T.anq[:, a_m:a_m + HALF], T.ans[:, a_m:a_m + HALF], True, True).then_inc(S.m_yn, 1)
+    TE.wait_ge(S.a_af, 2 * far_in)
+    TE.matmul_mx(ps[1][:, 0:HALF], T.w3q[:], T.w3s[:], T.afq[:], T.afs[:], True, True).then_inc(S.m_yf, 1)
+
+    V.wait_ge(S.l_xf, 16)
+    quant("xq", "xs", "xb", fo, fo + HALF, 4 * fo, S.q_xf)
+    V.wait_ge(S.l_w1a, 16)
+    for i in range(4):
+        if i == 3:
+            V.wait_ge(S.l_w1b, 16)
+        quant("w1q", "w1s", "w1b", 128 * i, 128 * i + 128, 512 * i, S["q_w1_%d" % i])
+    act(V, "hf", 3, 3, C1)
+    V.wait_ge(S.t_hf, 4)
+    quant("hfq", "hfs", "hf", 0, HALF, 0, S.q_hf)
+    V.wait_ge(S.l_xn, 16)
+    quant("xq", "xs", "xb", no, no + HALF, 4 * no, S.q_xn)
+    act(V, "hn", 1, 5, C1)
+    act(V, "hn", 3, 7, C1)
+    V.wait_ge(S.t_hn, 4)
+    quant("bnq", "bns", "hn", b_q, b_q + HALF, 0, S.q_hn)
+    V.wait_ge(S.l_w2, 16)
+    for i in range(4):
+        quant("w2q", "w2s", "w2b", 128 * i, 128 * i + 128, 512 * i, S["q_w2_%d" % i])
+    V.wait_ge(S.l_w3, 16)
+    quant("w3q", "w3s", "w3b", 0, 128, 0, S.q_w3)
+    act(V, "gn", 1, 1, C2)
+    act(V, "gn", 3, 3, C2)
+    V.wait_ge(S.t_gn, 4)
+    quant("anq", "ans", "gn", a_q, a_q + HALF, 0, S.q_gn)
+    act(V, "gf", 1, 5, C2)
+    act(V, "gf", 3, 7, C2)
+    V.wait_ge(S.t_gf, 4)
+    quant("gfq", "gfs", "gf", 0, HALF, 0, S.q_gf)
+    V.wait_ge(S.m_yn, 1)
+    V.tensor_copy(T.yn[:], ps[0][:, 0:HALF]).then_inc(S.c_yn, 1)
+    V.wait_ge(S.m_yf, 1)
+    V.tensor_copy(T.yf[:], ps[1][:, 0:HALF]).then_inc(S.c_yf, 1)
+
+    for i in (0, 1, 2):
+        act(SC, "hf", i, i, C1)
+    for i in (0, 2):
+        act(SC, "hn", i, 4 + i, C1)
+    for i in (0, 2):
+        act(SC, "gn", i, i, C2)
+    for i in (0, 2):
+        act(SC, "gf", i, 4 + i, C2)
+
+    SY.wait_ge(S.c_yn, 1)
+    SY.dma_start(T.y[:, no:no + HALF], T.yn[:]).then_inc(S.st_n, 16)
+    SY.wait_ge(S.c_yf, 1)
+    SY.dma_start(T.y[:, fo:fo + HALF], T.yf[:]).then_inc(S.st_f, 16)
+    SY.wait_ge(S.st_n, 16)
+    SY.wait_ge(S.st_f, 16)
+
+    sent = [0]
+
+    def to_relays(q, p, rq, rp):
+        for codes, src, dst, sem in ((True, q, rq, S[rq]), (False, p, rp, S[rp])):
+            tr = []
+            for i, d in enumerate(me_far):
+                r = relay[rank, d]
+                rid, pid, _ = topo.addr(r)
+                m = _hop1(topo, core, r, i, len(me_far))
+                a, b = T[src][:, RUN * i:RUN * i + RUN], T[dst][:]
+                if codes:
+                    a, b = a.bitcast(dt.uint8), b.bitcast(dt.uint8)
+                tr.append(RemoteDMATransfer(dst_ids=[DstId(rid=rid, pnc=pid)], dma_engine_mask=m, remote_sem=sem, srcs=[a], dsts=[b]))
+                sent[0] += len(_bits(m))
+            g.remote_dma_fused(tr, local_sem=S.sent)
+
+    def to_peer(q, p, c, land, sem):
+        sent[0] += _send(g, topo, core, cores[peer], near_mask, T[q][:, land:land + RUN].bitcast(dt.uint8),
+                         T[q][:, c:c + RUN].bitcast(dt.uint8), sem, S.sent)
+        sent[0] += _send(g, topo, core, cores[peer], near_mask, T[p][:, land:land + RUN], T[p][:, c:c + RUN], sem, S.sent)
+
+    g.wait_ge(S.q_hf, 1)
+    to_relays("hfq", "hfs", "rhq", "rhs")
+    g.wait_ge(S.q_hn, 1)
+    to_peer("bnq", "bns", b_out, b_land, S.a_bn)
+    g.wait_ge(S.q_gn, 1)
+    to_peer("anq", "ans", a_out, a_land, S.a_an)
+    g.wait_ge(S.q_gf, 1)
+    to_relays("gfq", "gfs", "rgq", "rgs")
+    g.wait_ge(S.sent, sent[0])

@@ -5,6 +5,8 @@ from concourse.mybir import dt, AluOpType, ActivationFunctionType
 SIM = 96
 RUN = 96
 HALF = 2 * RUN
+WIDE = 128
+PAD = WIDE - RUN
 C1 = float(np.float32(0.019))
 C2 = float(np.float32(0.029))
 F8, U8, BF, F32 = "float8_e4m3fn_x4", "uint8", "bfloat16", "float32"
@@ -17,29 +19,29 @@ SCRATCH = {
     "w2q": ("sbuf", [128, 512], F8), "w2s": ("sbuf", [128, 512], U8),
     "w3q": ("sbuf", [128, 128], F8), "w3s": ("sbuf", [128, 128], U8),
     "hf": ("sbuf", [128, 4 * HALF], BF), "hn": ("sbuf", [128, 4 * HALF], BF),
-    "gf": ("sbuf", [128, 4 * HALF], BF), "gn": ("sbuf", [128, 4 * HALF], BF),
+    "gt": ("sbuf", [128, 16 * RUN], BF),
     "hfq": ("sbuf", [128, HALF], F8), "hfs": ("sbuf", [128, HALF], U8),
-    "gfq": ("sbuf", [128, HALF], F8), "gfs": ("sbuf", [128, HALF], U8),
-    "bfq": ("sbuf", [128, HALF], F8), "bfs": ("sbuf", [128, HALF], U8),
-    "afq": ("sbuf", [128, HALF], F8), "afs": ("sbuf", [128, HALF], U8),
-    "bnq": ("sbuf", [128, 3 * RUN], F8), "bns": ("sbuf", [128, 3 * RUN], U8),
-    "anq": ("sbuf", [128, 3 * RUN], F8), "ans": ("sbuf", [128, 3 * RUN], U8),
-    "rhq": ("sbuf", [128, RUN], F8), "rhs": ("sbuf", [128, RUN], U8),
-    "rgq": ("sbuf", [128, RUN], F8), "rgs": ("sbuf", [128, RUN], U8),
-    "yn": ("sbuf", [128, HALF], F32), "yf": ("sbuf", [128, HALF], F32),
+    "g0q": ("sbuf", [128, WIDE], F8), "g0s": ("sbuf", [128, WIDE], U8),
+    "g1q": ("sbuf", [128, WIDE], F8), "g1s": ("sbuf", [128, WIDE], U8),
+    "bq": ("sbuf", [128, 5 * RUN], F8), "bs": ("sbuf", [128, 5 * RUN], U8),
+    "aq": ("sbuf", [128, 5 * RUN], F8), "as": ("sbuf", [128, 5 * RUN], U8),
+    "rhq": ("sbuf", [128, HALF], F8), "rhs": ("sbuf", [128, HALF], U8),
+    "rgq": ("sbuf", [128, HALF], F8), "rgs": ("sbuf", [128, HALF], U8),
+    "yn": ("sbuf", [128, HALF], F32), "y0": ("sbuf", [128, RUN], F32), "y1": ("sbuf", [128, RUN], F32),
 }
 for _k in range(8):
     SCRATCH["ps%d" % _k] = ("psum", [128, 512], F32)
 
 SEMAPHORES = (
-    ["l_xf", "l_xn", "l_w1a", "l_w1b", "l_w2", "l_w3"]
-    + ["q_xf", "q_xn", "q_w3", "q_hf", "q_hn", "q_gf", "q_gn"]
+    ["l_xf", "l_xn", "l_w1a", "l_w1b", "l_w1c", "l_w2", "l_w3"]
+    + ["q_xf", "q_xn", "q_w3", "q_hf", "q_hn", "q_gn", "q_g0", "q_g1"]
     + ["q_w1_%d" % i for i in range(4)] + ["q_w2_%d" % i for i in range(4)]
-    + ["m_%s%d" % (t, i) for t in ("hf", "hn", "gf", "gn") for i in range(4)] + ["m_yn", "m_yf"]
-    + ["t_hf", "t_hn", "t_gf", "t_gn"]
-    + ["rhq", "rhs", "rgq", "rgs"]
-    + ["a_bf", "a_bn", "a_af", "a_an"]
-    + ["c_yn", "c_yf", "sent", "st_n", "st_f"])
+    + ["m_%s_%d" % (t, i) for t in ("hf", "hn", "gn", "g0", "g1") for i in range(4)]
+    + ["m_yn", "m_y0", "m_y1"]
+    + ["t_hf", "t_hn", "t_gn", "t_g0", "t_g1"]
+    + ["rh", "rg0", "rg1"]
+    + ["a_bn", "a_b0", "a_b1", "a_an", "a_a0", "a_a1"]
+    + ["c_yn", "c_y0", "c_y1", "sent", "st_n", "st_0", "st_1"])
 
 
 def _bits(mask):
@@ -48,202 +50,192 @@ def _bits(mask):
 
 def _plan(T, topo):
     cores = list(T.cores)
-    far, relay = [], {}
+    far, near, step, relay = [], [], [], []
     for s, cs in enumerate(cores):
-        f = [d for d, cd in enumerate(cores) if d != s and not topo.may_write(cs, cd)]
-        cand = [c for c in range(SIM) if T.rank_of(c) is None and topo.chip(c) == topo.chip(cs)
-                and topo.die(c) == topo.die(cs) and all(topo.may_write(c, cores[d]) for d in f)]
+        f = [d for d, cd in enumerate(cores) if cd != cs and not topo.may_write(cs, cd)]
+        n = [d for d in range(len(cores)) if d not in f]
         far.append(f)
-        for i, d in enumerate(f):
-            relay[s, d] = cand[i]
-    return cores, far, relay
+        near.append(n)
+        step.append([f[(t + n.index(s)) % len(f)] for t in range(len(f))])
+        relay.append([c for c in range(SIM) if T.rank_of(c) is None and topo.chip(c) == topo.chip(cs)
+                      and topo.die(c) == topo.die(cs) and all(topo.may_write(c, cores[d]) for d in f)][:2])
+    return cores, far, near, step, relay
 
 
-def _send(g, topo, core, dst, mask, out, in_, rsem, lsem):
+def _send(g, topo, core, dst, out, in_, rsem, lsem):
     rid, pid, _ = topo.addr(dst)
+    mask = topo.mask(core, dst)
     g.remote_dma(out, in_, rsem, lsem, pid, rid, mask)
     return len(_bits(mask))
 
 
-def _relay_program(g, core, T, topo, cores, far, s, d):
+def _cols(T, name, kind, a, b):
+    v = T[name + "qs"[kind]][:, a:b]
+    return v.bitcast(dt.uint8) if kind == 0 else v
+
+
+B_FAR = (3 * RUN, 4 * RUN)
+A_FAR = (RUN, 0)
+
+
+def _relay_program(g, core, T, topo, cores, far, step, s, kind):
     S = T.sem
-    i = far[d].index(s)
-    a, b = RUN * i, RUN * i + RUN
-    dst = cores[d]
-    n_in = _hop1(topo, cores[s], core, far[s].index(d), len(far[s]))
-    n_in = len(_bits(n_in))
-    out_mask = topo.mask(core, dst)
+    n_in = len(_bits(topo.mask(cores[s], core)))
     sent = 0
-    for q, p, dq, dp, sem in (("rhq", "rhs", "bfq", "bfs", S.a_bf), ("rgq", "rgs", "afq", "afs", S.a_af)):
-        g.wait_ge(S[q], n_in)
-        sent += _send(g, topo, core, dst, out_mask, T[dq][:, a:b].bitcast(dt.uint8), T[q][:].bitcast(dt.uint8), sem, S.sent)
-        g.wait_ge(S[p], n_in)
-        sent += _send(g, topo, core, dst, out_mask, T[dp][:, a:b], T[p][:], sem, S.sent)
+    g.wait_ge(S.rh, n_in)
+    for t, d in enumerate(step[s]):
+        k = RUN * far[s].index(d)
+        sent += _send(g, topo, core, cores[d], _cols(T, "b", kind, B_FAR[t], B_FAR[t] + RUN),
+                      _cols(T, "rh", kind, k, k + RUN), S["a_b%d" % t], S.sent)
+    for t, d in enumerate(step[s]):
+        g.wait_ge(S["rg%d" % t], n_in)
+        sent += _send(g, topo, core, cores[d], _cols(T, "a", kind, A_FAR[t], A_FAR[t] + RUN),
+                      _cols(T, "rg", kind, RUN * t, RUN * t + RUN), S["a_a%d" % t], S.sent)
     g.wait_ge(S.sent, sent)
 
 
-def _hop1(topo, src, relay, i, parts):
-    b = _bits(topo.mask(src, relay))
-    n = len(b) // parts
-    return sum(b[i * n:i * n + n])
-
-
 def rank_program(g, core, T, topo):
-    cores, far, relay = _plan(T, topo)
+    cores, far, near, step, relay = _plan(T, topo)
     rank = T.rank_of(core)
     S = T.sem
     if rank is None:
-        for (s, d), c in relay.items():
-            if c == core:
-                _relay_program(g, core, T, topo, cores, far, s, d)
+        for s, pair in enumerate(relay):
+            if core in pair:
+                _relay_program(g, core, T, topo, cores, far, step, s, pair.index(core))
         return
 
-    me_far = far[rank]
-    group = [r for r in range(len(cores)) if r not in me_far]
-    pos = group.index(rank)
-    peer = group[1 - pos]
-    fo, no = RUN * me_far[0], RUN * group[0]
+    me_far, me_step = far[rank], step[rank]
+    peer = [r for r in near[rank] if r != rank][0]
+    fo = RUN * me_far[0]
     V, SC, TE, SY = g.vector, g.scalar, g.tensor, g.sync
     relu = ActivationFunctionType.Relu
     ps = [T["ps%d" % k] for k in range(8)]
 
-    SY.dma_start(T.xb[:, 4 * fo:4 * fo + 4 * HALF], T.x[:, 4 * fo:4 * fo + 4 * HALF]).then_inc(S.l_xf, 16)
-    SC.dma_start(T.w1b[:, 0:1536], T.w1[:, 0:1536]).then_inc(S.l_w1a, 16)
-    SY.dma_start(T.w1b[:, 1536:2048], T.w1[:, 1536:2048]).then_inc(S.l_w1b, 16)
-    SY.dma_start(T.xb[:, 4 * no:4 * no + 4 * HALF], T.x[:, 4 * no:4 * no + 4 * HALF]).then_inc(S.l_xn, 16)
+    SY.dma_start(T.xb[:, 0:4 * HALF], T.x[:, 4 * fo:4 * fo + 4 * HALF]).then_inc(S.l_xf, 16)
+    SC.dma_start(T.w1b[:, 0:1024], T.w1[:, 0:1024]).then_inc(S.l_w1a, 16)
+    SY.dma_start(T.w1b[:, 1024:1536], T.w1[:, 1024:1536]).then_inc(S.l_w1b, 16)
+    SY.dma_start(T.w1b[:, 1536:2048], T.w1[:, 1536:2048]).then_inc(S.l_w1c, 16)
+    for k, r in ((2, peer), (3, rank)):
+        SY.dma_start(T.xb[:, 4 * RUN * k:4 * RUN * (k + 1)], T.x[:, 4 * RUN * r:4 * RUN * (r + 1)]).then_inc(S.l_xn, 16)
     SY.dma_start(T.w2b[:], T.w2[:]).then_inc(S.l_w2, 16)
     SY.dma_start(T.w3b[:], T.w3[:]).then_inc(S.l_w3, 16)
 
-    def quant(q, p, src, c0, c1, e0, sem):
-        V.quantize_mx(T[q][:, c0:c1], T[p][:, c0:c1], T[src][:, e0:e0 + 4 * (c1 - c0)]).then_inc(sem, 1)
+    def quant(q, c0, c1, src, e0, sem):
+        V.quantize_mx(T[q + "q"][:, c0:c1], T[q + "s"][:, c0:c1], T[src][:, 4 * e0:4 * (e0 + c1 - c0)]).then_inc(sem, 1)
 
-    def act(eng, tile, i, bank, c):
-        out, src = T[tile][:, i:4 * HALF:4], ps[bank][:, 0:HALF]
-        eng.wait_ge(S["m_%s%d" % (tile, i)], 1)
+    PART = {"hf": ("hf", 0, HALF, 0, 0, C1), "hn": ("hn", 0, HALF, 0, 4, C1), "gn": ("gt", 0, HALF, 0, 0, C2),
+            "g0": ("gt", HALF, RUN, PAD, 4, C2), "g1": ("gt", HALF + RUN, RUN, PAD, 0, C2)}
+
+    def act(eng, part, i):
+        tile, c0, n, p0, bank, c = PART[part]
+        out, src = T[tile][:, 4 * c0 + i:4 * (c0 + n):4], ps[bank + i][:, p0:p0 + n]
+        eng.wait_ge(S["m_%s_%d" % (part, i)], 1)
         if eng is SC:
-            SC.activation(out, src, relu, scale=c).then_inc(S["t_" + tile], 1)
+            SC.activation(out, src, relu, scale=c).then_inc(S["t_" + part], 1)
         else:
-            V.tensor_scalar(out, src, 0.0, c, AluOpType.max, AluOpType.mult).then_inc(S["t_" + tile], 1)
+            V.tensor_scalar(out, src, 0.0, c, AluOpType.max, AluOpType.mult).then_inc(S["t_" + part], 1)
 
-    def product(tile, i, bank, w, q, p, c0):
-        TE.matmul_mx(ps[bank][:, 0:HALF], T[w + "q"][:, 128 * i:128 * i + 128], T[w + "s"][:, 128 * i:128 * i + 128],
-                     T[q][:, c0:c0 + HALF], T[p][:, c0:c0 + HALF], True, True).then_inc(S["m_%s%d" % (tile, i)], 1)
+    def product(part, i, w, q, a, b):
+        TE.matmul_mx(ps[PART[part][4] + i][:, 0:b - a], T[w + "q"][:, 128 * i:128 * i + 128], T[w + "s"][:, 128 * i:128 * i + 128],
+                     T[q + "q"][:, a:b], T[q + "s"][:, a:b], True, True).then_inc(S["m_%s_%d" % (part, i)], 1)
 
-    b_q = RUN if pos == 0 else 0
-    b_m = 0 if pos == 0 else RUN
-    a_q, a_m = b_m, b_q
-    b_out = 2 * RUN if pos == 0 else 0
-    a_out = 0 if pos == 0 else 2 * RUN
-    b_land = 2 * RUN if pos == 0 else 0
-    a_land = 0 if pos == 0 else 2 * RUN
+    def final(bank, a, b, sem):
+        TE.matmul_mx(ps[bank][:, 0:b - a], T.w3q[:], T.w3s[:], T["aq"][:, a:b], T["as"][:, a:b], True, True).then_inc(sem, 1)
+
+    near_in = 2 * len(_bits(topo.mask(cores[peer], core)))
+    far_in = [sum(len(_bits(topo.mask(c, core))) for c in relay[s]) for s in me_step]
 
     TE.wait_ge(S.q_xf, 1)
     for i in range(4):
         TE.wait_ge(S["q_w1_%d" % i], 1)
-        product("hf", i, i, "w1", "xq", "xs", fo)
+        product("hf", i, "w1", "x", 0, HALF)
     TE.wait_ge(S.q_xn, 1)
     for i in range(4):
-        product("hn", i, 4 + i, "w1", "xq", "xs", no)
-
-    near_mask = topo.mask(core, cores[peer])
-    near_in = len(_bits(topo.mask(cores[peer], core)))
-    far_in = sum(len(_bits(topo.mask(relay[s, rank], core))) for s in me_far)
-
+        product("hn", i, "w1", "x", HALF, 2 * HALF)
     TE.wait_ge(S.t_hf, 4)
     TE.wait_ge(S.q_hn, 1)
-    TE.wait_ge(S.a_bn, 2 * near_in)
+    TE.wait_ge(S.a_bn, near_in)
     for i in range(4):
         TE.wait_ge(S["q_w2_%d" % i], 1)
-        product("gn", i, i, "w2", "bnq", "bns", b_m)
-    TE.wait_ge(S.t_hn, 4)
-    TE.wait_ge(S.a_bf, 2 * far_in)
-    for i in range(4):
-        product("gf", i, 4 + i, "w2", "bfq", "bfs", 0)
+        product("gn", i, "w2", "b", RUN, 3 * RUN)
+    for t, free in enumerate((S.t_hn, S.t_gn)):
+        TE.wait_ge(free, 4)
+        TE.wait_ge(S["a_b%d" % t], far_in[t])
+        for i in range(4):
+            product("g%d" % t, i, "w2", "b", B_FAR[t] - PAD, B_FAR[t] + RUN)
+    TE.wait_ge(S.t_g0, 4)
     TE.wait_ge(S.q_w3, 1)
-    TE.wait_ge(S.t_gn, 4)
     TE.wait_ge(S.q_gn, 1)
-    TE.wait_ge(S.a_an, 2 * near_in)
-    TE.matmul_mx(ps[0][:, 0:HALF], T.w3q[:], T.w3s[:], T.anq[:, a_m:a_m + HALF], T.ans[:, a_m:a_m + HALF], True, True).then_inc(S.m_yn, 1)
-    TE.wait_ge(S.a_af, 2 * far_in)
-    TE.matmul_mx(ps[1][:, 0:HALF], T.w3q[:], T.w3s[:], T.afq[:], T.afs[:], True, True).then_inc(S.m_yf, 1)
+    TE.wait_ge(S.a_an, near_in)
+    final(4, 2 * RUN, 4 * RUN, S.m_yn)
+    for t in range(2):
+        TE.wait_ge(S["a_a%d" % t], far_in[t])
+        final(5 + t, A_FAR[t], A_FAR[t] + WIDE, S["m_y%d" % t])
 
     V.wait_ge(S.l_xf, 16)
-    quant("xq", "xs", "xb", fo, fo + HALF, 4 * fo, S.q_xf)
-    V.wait_ge(S.l_w1a, 16)
-    for i in range(4):
-        if i == 3:
-            V.wait_ge(S.l_w1b, 16)
-        quant("w1q", "w1s", "w1b", 128 * i, 128 * i + 128, 512 * i, S["q_w1_%d" % i])
-    act(V, "hf", 3, 3, C1)
+    quant("x", 0, HALF, "xb", 0, S.q_xf)
+    for i, load in enumerate((S.l_w1a, None, S.l_w1b, S.l_w1c)):
+        if load is not None:
+            V.wait_ge(load, 16)
+        quant("w1", 128 * i, 128 * i + 128, "w1b", 128 * i, S["q_w1_%d" % i])
+    act(V, "hf", 3)
     V.wait_ge(S.t_hf, 4)
-    quant("hfq", "hfs", "hf", 0, HALF, 0, S.q_hf)
-    V.wait_ge(S.l_xn, 16)
-    quant("xq", "xs", "xb", no, no + HALF, 4 * no, S.q_xn)
-    act(V, "hn", 1, 5, C1)
-    act(V, "hn", 3, 7, C1)
+    quant("hf", 0, HALF, "hf", 0, S.q_hf)
+    V.wait_ge(S.l_xn, 32)
+    quant("x", HALF, 2 * HALF, "xb", HALF, S.q_xn)
+    act(V, "hn", 1)
+    act(V, "hn", 3)
     V.wait_ge(S.t_hn, 4)
-    quant("bnq", "bns", "hn", b_q, b_q + HALF, 0, S.q_hn)
+    quant("b", 0, HALF, "hn", 0, S.q_hn)
     V.wait_ge(S.l_w2, 16)
     for i in range(4):
-        quant("w2q", "w2s", "w2b", 128 * i, 128 * i + 128, 512 * i, S["q_w2_%d" % i])
+        quant("w2", 128 * i, 128 * i + 128, "w2b", 128 * i, S["q_w2_%d" % i])
     V.wait_ge(S.l_w3, 16)
-    quant("w3q", "w3s", "w3b", 0, 128, 0, S.q_w3)
-    act(V, "gn", 1, 1, C2)
-    act(V, "gn", 3, 3, C2)
+    quant("w3", 0, 128, "w3b", 0, S.q_w3)
+    act(V, "gn", 1)
+    act(V, "gn", 3)
     V.wait_ge(S.t_gn, 4)
-    quant("anq", "ans", "gn", a_q, a_q + HALF, 0, S.q_gn)
-    act(V, "gf", 1, 5, C2)
-    act(V, "gf", 3, 7, C2)
-    V.wait_ge(S.t_gf, 4)
-    quant("gfq", "gfs", "gf", 0, HALF, 0, S.q_gf)
+    quant("a", 3 * RUN, 5 * RUN, "gt", 0, S.q_gn)
+    for t in range(2):
+        act(V, "g%d" % t, 1)
+        act(V, "g%d" % t, 3)
+        V.wait_ge(S["t_g%d" % t], 4)
+        quant("g%d" % t, 0, WIDE, "gt", HALF + RUN * t - PAD, S["q_g%d" % t])
     V.wait_ge(S.m_yn, 1)
-    V.tensor_copy(T.yn[:], ps[0][:, 0:HALF]).then_inc(S.c_yn, 1)
-    V.wait_ge(S.m_yf, 1)
-    V.tensor_copy(T.yf[:], ps[1][:, 0:HALF]).then_inc(S.c_yf, 1)
+    V.tensor_copy(T.yn[:], ps[4][:, 0:HALF]).then_inc(S.c_yn, 1)
+    for t in range(2):
+        V.wait_ge(S["m_y%d" % t], 1)
+        V.tensor_copy(T["y%d" % t][:], ps[5 + t][:, 0:RUN]).then_inc(S["c_y%d" % t], 1)
 
     for i in (0, 1, 2):
-        act(SC, "hf", i, i, C1)
-    for i in (0, 2):
-        act(SC, "hn", i, 4 + i, C1)
-    for i in (0, 2):
-        act(SC, "gn", i, i, C2)
-    for i in (0, 2):
-        act(SC, "gf", i, 4 + i, C2)
+        act(SC, "hf", i)
+    for part in ("hn", "gn", "g0", "g1"):
+        for i in (0, 2):
+            act(SC, part, i)
 
     SY.wait_ge(S.c_yn, 1)
-    SY.dma_start(T.y[:, no:no + HALF], T.yn[:]).then_inc(S.st_n, 16)
-    SY.wait_ge(S.c_yf, 1)
-    SY.dma_start(T.y[:, fo:fo + HALF], T.yf[:]).then_inc(S.st_f, 16)
-    SY.wait_ge(S.st_n, 16)
-    SY.wait_ge(S.st_f, 16)
+    for k, r in enumerate((peer, rank)):
+        SY.dma_start(T.y[:, RUN * r:RUN * r + RUN], T.yn[:, RUN * k:RUN * k + RUN]).then_inc(S.st_n, 16)
+    for t, d in enumerate(me_step):
+        SY.wait_ge(S["c_y%d" % t], 1)
+        SY.dma_start(T.y[:, RUN * d:RUN * d + RUN], T["y%d" % t][:]).then_inc(S["st_%d" % t], 16)
+    SY.wait_ge(S.st_n, 32)
+    SY.wait_ge(S.st_0, 16)
+    SY.wait_ge(S.st_1, 16)
 
-    sent = [0]
-
-    def to_relays(q, p, rq, rp):
-        for codes, src, dst, sem in ((True, q, rq, S[rq]), (False, p, rp, S[rp])):
-            tr = []
-            for i, d in enumerate(me_far):
-                r = relay[rank, d]
-                rid, pid, _ = topo.addr(r)
-                m = _hop1(topo, core, r, i, len(me_far))
-                a, b = T[src][:, RUN * i:RUN * i + RUN], T[dst][:]
-                if codes:
-                    a, b = a.bitcast(dt.uint8), b.bitcast(dt.uint8)
-                tr.append(RemoteDMATransfer(dst_ids=[DstId(rid=rid, pnc=pid)], dma_engine_mask=m, remote_sem=sem, srcs=[a], dsts=[b]))
-                sent[0] += len(_bits(m))
-            g.remote_dma_fused(tr, local_sem=S.sent)
-
-    def to_peer(q, p, c, land, sem):
-        sent[0] += _send(g, topo, core, cores[peer], near_mask, T[q][:, land:land + RUN].bitcast(dt.uint8),
-                         T[q][:, c:c + RUN].bitcast(dt.uint8), sem, S.sent)
-        sent[0] += _send(g, topo, core, cores[peer], near_mask, T[p][:, land:land + RUN], T[p][:, c:c + RUN], sem, S.sent)
-
+    sent = 0
     g.wait_ge(S.q_hf, 1)
-    to_relays("hfq", "hfs", "rhq", "rhs")
+    for kind in range(2):
+        sent += _send(g, topo, core, relay[rank][kind], _cols(T, "rh", kind, 0, HALF), _cols(T, "hf", kind, 0, HALF), S.rh, S.sent)
     g.wait_ge(S.q_hn, 1)
-    to_peer("bnq", "bns", b_out, b_land, S.a_bn)
+    for kind in range(2):
+        sent += _send(g, topo, core, cores[peer], _cols(T, "b", kind, 2 * RUN, 3 * RUN), _cols(T, "b", kind, 0, RUN), S.a_bn, S.sent)
     g.wait_ge(S.q_gn, 1)
-    to_peer("anq", "ans", a_out, a_land, S.a_an)
-    g.wait_ge(S.q_gf, 1)
-    to_relays("gfq", "gfs", "rgq", "rgs")
-    g.wait_ge(S.sent, sent[0])
+    for kind in range(2):
+        sent += _send(g, topo, core, cores[peer], _cols(T, "a", kind, 2 * RUN, 3 * RUN), _cols(T, "a", kind, 4 * RUN, 5 * RUN), S.a_an, S.sent)
+    for t in range(2):
+        g.wait_ge(S["q_g%d" % t], 1)
+        for kind in range(2):
+            sent += _send(g, topo, core, relay[rank][kind], _cols(T, "rg", kind, RUN * t, RUN * t + RUN),
+                          _cols(T, "g%d" % t, kind, PAD, WIDE), S["rg%d" % t], S.sent)
+    g.wait_ge(S.sent, sent)

import numpy as np
from concourse.bass import DstId, RemoteDMATransfer
from concourse.mybir import dt, AluOpType, ActivationFunctionType

SIM = 96
RUN = 96
HALF = 2 * RUN
WIDE = 128
PAD = WIDE - RUN
C1 = float(np.float32(0.019))
C2 = float(np.float32(0.029))
F8, U8, BF, F32 = "float8_e4m3fn_x4", "uint8", "bfloat16", "float32"

SCRATCH = {
    "xb": ("sbuf", [128, 1536], BF), "w1b": ("sbuf", [128, 2048], BF),
    "w2b": ("sbuf", [128, 2048], BF), "w3b": ("sbuf", [128, 512], BF),
    "xq": ("sbuf", [128, 384], F8), "xs": ("sbuf", [128, 384], U8),
    "w1q": ("sbuf", [128, 512], F8), "w1s": ("sbuf", [128, 512], U8),
    "w2q": ("sbuf", [128, 512], F8), "w2s": ("sbuf", [128, 512], U8),
    "w3q": ("sbuf", [128, 128], F8), "w3s": ("sbuf", [128, 128], U8),
    "hf": ("sbuf", [128, 4 * HALF], BF), "hn": ("sbuf", [128, 4 * HALF], BF),
    "gt": ("sbuf", [128, 16 * RUN], BF),
    "hfq": ("sbuf", [128, HALF], F8), "hfs": ("sbuf", [128, HALF], U8),
    "g0q": ("sbuf", [128, WIDE], F8), "g0s": ("sbuf", [128, WIDE], U8),
    "g1q": ("sbuf", [128, WIDE], F8), "g1s": ("sbuf", [128, WIDE], U8),
    "bq": ("sbuf", [128, 5 * RUN], F8), "bs": ("sbuf", [128, 5 * RUN], U8),
    "aq": ("sbuf", [128, 5 * RUN], F8), "as": ("sbuf", [128, 5 * RUN], U8),
    "rhq": ("sbuf", [128, HALF], F8), "rhs": ("sbuf", [128, HALF], U8),
    "rgq": ("sbuf", [128, HALF], F8), "rgs": ("sbuf", [128, HALF], U8),
    "yn": ("sbuf", [128, HALF], F32), "y0": ("sbuf", [128, RUN], F32), "y1": ("sbuf", [128, RUN], F32),
}
for _k in range(8):
    SCRATCH["ps%d" % _k] = ("psum", [128, 512], F32)

SEMAPHORES = (
    ["l_xf", "l_xn", "l_w1a", "l_w1b", "l_w1c", "l_w2", "l_w3"]
    + ["q_xf", "q_xn", "q_w3", "q_hf", "q_hn", "q_gn", "q_g0", "q_g1"]
    + ["q_w1_%d" % i for i in range(4)] + ["q_w2_%d" % i for i in range(4)]
    + ["m_%s_%d" % (t, i) for t in ("hf", "hn", "gn", "g0", "g1") for i in range(4)]
    + ["m_yn", "m_y0", "m_y1"]
    + ["t_hf", "t_hn", "t_gn", "t_g0", "t_g1"]
    + ["rh", "rg0", "rg1"]
    + ["a_bn", "a_b0", "a_b1", "a_an", "a_a0", "a_a1"]
    + ["c_yn", "c_y0", "c_y1", "sent", "st_n", "st_0", "st_1"])


def _bits(mask):
    return [1 << k for k in range(mask.bit_length()) if mask >> k & 1]


def _plan(T, topo):
    cores = list(T.cores)
    far, near, step, relay = [], [], [], []
    for s, cs in enumerate(cores):
        f = [d for d, cd in enumerate(cores) if cd != cs and not topo.may_write(cs, cd)]
        n = [d for d in range(len(cores)) if d not in f]
        far.append(f)
        near.append(n)
        step.append([f[(t + n.index(s)) % len(f)] for t in range(len(f))])
        relay.append([c for c in range(SIM) if T.rank_of(c) is None and topo.chip(c) == topo.chip(cs)
                      and topo.die(c) == topo.die(cs) and all(topo.may_write(c, cores[d]) for d in f)][:2])
    return cores, far, near, step, relay


def _send(g, topo, core, dst, out, in_, rsem, lsem):
    rid, pid, _ = topo.addr(dst)
    mask = topo.mask(core, dst)
    g.remote_dma(out, in_, rsem, lsem, pid, rid, mask)
    return len(_bits(mask))


def _cols(T, name, kind, a, b):
    v = T[name + "qs"[kind]][:, a:b]
    return v.bitcast(dt.uint8) if kind == 0 else v


B_FAR = (3 * RUN, 4 * RUN)
A_FAR = (RUN, 0)


def _relay_program(g, core, T, topo, cores, far, step, s, kind):
    S = T.sem
    n_in = len(_bits(topo.mask(cores[s], core)))
    sent = 0
    g.wait_ge(S.rh, n_in)
    for t, d in enumerate(step[s]):
        k = RUN * far[s].index(d)
        sent += _send(g, topo, core, cores[d], _cols(T, "b", kind, B_FAR[t], B_FAR[t] + RUN),
                      _cols(T, "rh", kind, k, k + RUN), S["a_b%d" % t], S.sent)
    for t, d in enumerate(step[s]):
        g.wait_ge(S["rg%d" % t], n_in)
        sent += _send(g, topo, core, cores[d], _cols(T, "a", kind, A_FAR[t], A_FAR[t] + RUN),
                      _cols(T, "rg", kind, RUN * t, RUN * t + RUN), S["a_a%d" % t], S.sent)
    g.wait_ge(S.sent, sent)


def rank_program(g, core, T, topo):
    cores, far, near, step, relay = _plan(T, topo)
    rank = T.rank_of(core)
    S = T.sem
    if rank is None:
        for s, pair in enumerate(relay):
            if core in pair:
                _relay_program(g, core, T, topo, cores, far, step, s, pair.index(core))
        return

    me_far, me_step = far[rank], step[rank]
    peer = [r for r in near[rank] if r != rank][0]
    fo = RUN * me_far[0]
    V, SC, TE, SY = g.vector, g.scalar, g.tensor, g.sync
    relu = ActivationFunctionType.Relu
    ps = [T["ps%d" % k] for k in range(8)]

    SY.dma_start(T.xb[:, 0:4 * HALF], T.x[:, 4 * fo:4 * fo + 4 * HALF]).then_inc(S.l_xf, 16)
    SC.dma_start(T.w1b[:, 0:1024], T.w1[:, 0:1024]).then_inc(S.l_w1a, 16)
    SY.dma_start(T.w1b[:, 1024:1536], T.w1[:, 1024:1536]).then_inc(S.l_w1b, 16)
    SY.dma_start(T.w1b[:, 1536:2048], T.w1[:, 1536:2048]).then_inc(S.l_w1c, 16)
    for k, r in ((2, peer), (3, rank)):
        SY.dma_start(T.xb[:, 4 * RUN * k:4 * RUN * (k + 1)], T.x[:, 4 * RUN * r:4 * RUN * (r + 1)]).then_inc(S.l_xn, 16)
    SY.dma_start(T.w2b[:], T.w2[:]).then_inc(S.l_w2, 16)
    SY.dma_start(T.w3b[:], T.w3[:]).then_inc(S.l_w3, 16)

    def quant(q, c0, c1, src, e0, sem):
        V.quantize_mx(T[q + "q"][:, c0:c1], T[q + "s"][:, c0:c1], T[src][:, 4 * e0:4 * (e0 + c1 - c0)]).then_inc(sem, 1)

    PART = {"hf": ("hf", 0, HALF, 0, 0, C1), "hn": ("hn", 0, HALF, 0, 4, C1), "gn": ("gt", 0, HALF, 0, 0, C2),
            "g0": ("gt", HALF, RUN, PAD, 4, C2), "g1": ("gt", HALF + RUN, RUN, PAD, 0, C2)}

    def act(eng, part, i):
        tile, c0, n, p0, bank, c = PART[part]
        out, src = T[tile][:, 4 * c0 + i:4 * (c0 + n):4], ps[bank + i][:, p0:p0 + n]
        eng.wait_ge(S["m_%s_%d" % (part, i)], 1)
        if eng is SC:
            SC.activation(out, src, relu, scale=c).then_inc(S["t_" + part], 1)
        else:
            V.tensor_scalar(out, src, 0.0, c, AluOpType.max, AluOpType.mult).then_inc(S["t_" + part], 1)

    def product(part, i, w, q, a, b):
        TE.matmul_mx(ps[PART[part][4] + i][:, 0:b - a], T[w + "q"][:, 128 * i:128 * i + 128], T[w + "s"][:, 128 * i:128 * i + 128],
                     T[q + "q"][:, a:b], T[q + "s"][:, a:b], True, True).then_inc(S["m_%s_%d" % (part, i)], 1)

    def final(bank, a, b, sem):
        TE.matmul_mx(ps[bank][:, 0:b - a], T.w3q[:], T.w3s[:], T["aq"][:, a:b], T["as"][:, a:b], True, True).then_inc(sem, 1)

    near_in = 2 * len(_bits(topo.mask(cores[peer], core)))
    far_in = [sum(len(_bits(topo.mask(c, core))) for c in relay[s]) for s in me_step]

    TE.wait_ge(S.q_xf, 1)
    for i in range(4):
        TE.wait_ge(S["q_w1_%d" % i], 1)
        product("hf", i, "w1", "x", 0, HALF)
    TE.wait_ge(S.q_xn, 1)
    for i in range(4):
        product("hn", i, "w1", "x", HALF, 2 * HALF)
    TE.wait_ge(S.t_hf, 4)
    TE.wait_ge(S.q_hn, 1)
    TE.wait_ge(S.a_bn, near_in)
    for i in range(4):
        TE.wait_ge(S["q_w2_%d" % i], 1)
        product("gn", i, "w2", "b", RUN, 3 * RUN)
    for t, free in enumerate((S.t_hn, S.t_gn)):
        TE.wait_ge(free, 4)
        TE.wait_ge(S["a_b%d" % t], far_in[t])
        for i in range(4):
            product("g%d" % t, i, "w2", "b", B_FAR[t] - PAD, B_FAR[t] + RUN)
    TE.wait_ge(S.t_g0, 4)
    TE.wait_ge(S.q_w3, 1)
    TE.wait_ge(S.q_gn, 1)
    TE.wait_ge(S.a_an, near_in)
    final(4, 2 * RUN, 4 * RUN, S.m_yn)
    for t in range(2):
        TE.wait_ge(S["a_a%d" % t], far_in[t])
        final(5 + t, A_FAR[t], A_FAR[t] + WIDE, S["m_y%d" % t])

    V.wait_ge(S.l_xf, 16)
    quant("x", 0, HALF, "xb", 0, S.q_xf)
    for i, load in enumerate((S.l_w1a, None, S.l_w1b, S.l_w1c)):
        if load is not None:
            V.wait_ge(load, 16)
        quant("w1", 128 * i, 128 * i + 128, "w1b", 128 * i, S["q_w1_%d" % i])
    act(V, "hf", 3)
    V.wait_ge(S.t_hf, 4)
    quant("hf", 0, HALF, "hf", 0, S.q_hf)
    V.wait_ge(S.l_xn, 32)
    quant("x", HALF, 2 * HALF, "xb", HALF, S.q_xn)
    act(V, "hn", 1)
    act(V, "hn", 3)
    V.wait_ge(S.t_hn, 4)
    quant("b", 0, HALF, "hn", 0, S.q_hn)
    V.wait_ge(S.l_w2, 16)
    for i in range(4):
        quant("w2", 128 * i, 128 * i + 128, "w2b", 128 * i, S["q_w2_%d" % i])
    V.wait_ge(S.l_w3, 16)
    quant("w3", 0, 128, "w3b", 0, S.q_w3)
    act(V, "gn", 1)
    act(V, "gn", 3)
    V.wait_ge(S.t_gn, 4)
    quant("a", 3 * RUN, 5 * RUN, "gt", 0, S.q_gn)
    for t in range(2):
        act(V, "g%d" % t, 1)
        act(V, "g%d" % t, 3)
        V.wait_ge(S["t_g%d" % t], 4)
        quant("g%d" % t, 0, WIDE, "gt", HALF + RUN * t - PAD, S["q_g%d" % t])
    V.wait_ge(S.m_yn, 1)
    V.tensor_copy(T.yn[:], ps[4][:, 0:HALF]).then_inc(S.c_yn, 1)
    for t in range(2):
        V.wait_ge(S["m_y%d" % t], 1)
        V.tensor_copy(T["y%d" % t][:], ps[5 + t][:, 0:RUN]).then_inc(S["c_y%d" % t], 1)

    for i in (0, 1, 2):
        act(SC, "hf", i)
    for part in ("hn", "gn", "g0", "g1"):
        for i in (0, 2):
            act(SC, part, i)

    SY.wait_ge(S.c_yn, 1)
    for k, r in enumerate((peer, rank)):
        SY.dma_start(T.y[:, RUN * r:RUN * r + RUN], T.yn[:, RUN * k:RUN * k + RUN]).then_inc(S.st_n, 16)
    for t, d in enumerate(me_step):
        SY.wait_ge(S["c_y%d" % t], 1)
        SY.dma_start(T.y[:, RUN * d:RUN * d + RUN], T["y%d" % t][:]).then_inc(S["st_%d" % t], 16)
    SY.wait_ge(S.st_n, 32)
    SY.wait_ge(S.st_0, 16)
    SY.wait_ge(S.st_1, 16)

    sent = 0
    g.wait_ge(S.q_hf, 1)
    for kind in range(2):
        sent += _send(g, topo, core, relay[rank][kind], _cols(T, "rh", kind, 0, HALF), _cols(T, "hf", kind, 0, HALF), S.rh, S.sent)
    g.wait_ge(S.q_hn, 1)
    for kind in range(2):
        sent += _send(g, topo, core, cores[peer], _cols(T, "b", kind, 2 * RUN, 3 * RUN), _cols(T, "b", kind, 0, RUN), S.a_bn, S.sent)
    g.wait_ge(S.q_gn, 1)
    for kind in range(2):
        sent += _send(g, topo, core, cores[peer], _cols(T, "a", kind, 2 * RUN, 3 * RUN), _cols(T, "a", kind, 4 * RUN, 5 * RUN), S.a_an, S.sent)
    for t in range(2):
        g.wait_ge(S["q_g%d" % t], 1)
        for kind in range(2):
            sent += _send(g, topo, core, relay[rank][kind], _cols(T, "rg", kind, RUN * t, RUN * t + RUN),
                          _cols(T, "g%d" % t, kind, PAD, WIDE), S["rg%d" % t], S.sent)
    g.wait_ge(S.sent, sent)
